import numpy as np
import ml_dtypes


def mxq(x, axis, fmt="e4m3"):
    dtype, down = {"e4m3": (ml_dtypes.float8_e4m3fn, 7), "e5m2": (ml_dtypes.float8_e5m2, 14)}[fmt]
    v = np.moveaxis(np.asarray(x, np.float32).astype(ml_dtypes.bfloat16).astype(np.float64), axis, -1)
    blocks = v.reshape(v.shape[:-1] + (-1, 32))
    amax = np.abs(blocks).max(-1, keepdims=True)
    byte = np.maximum(np.where(amax > 0, np.frexp(amax)[1] - 1 + 127, 0) - down, 1)
    scale = np.exp2(byte - 127.0)
    codes = (blocks / scale).astype(np.float32).astype(dtype).astype(np.float64)
    return np.moveaxis((codes * scale).reshape(v.shape), -1, axis)


WIDE = False


def mx_kscale(k):
    if not WIDE:
        return np.ones(k)
    levels = np.array([10, -10, 5, -5, 0])
    if k % 512:
        return np.exp2(np.random.permutation(np.resize(levels, k // 32))).repeat(32)
    a = np.empty((k // 512, 16))
    for p in range(k // 512):
        a[p, :8] = np.random.permutation(np.resize(levels, 8))
        for g in range(8):
            far = levels[np.abs(levels - a[p, g]) >= 10]
            a[p, g + 8] = far[np.random.randint(len(far))]
    return np.exp2(a.ravel()).repeat(32)


def f64(x):
    return np.asarray(x).astype(np.float64)


def striped(idx):
    return np.tile(np.asarray(idx).reshape(-1, 16).T, (8, 1)).astype(np.uint16)


def unstriped(offs):
    return offs[:16].T.reshape(-1).astype(np.int64)


E2M1 = np.array([0.0, 0.5, 1.0, 1.5, 2.0, 3.0, 4.0, 6.0, -0.0, -0.5, -1.0, -1.5, -2.0, -3.0, -4.0, -6.0])


def pack_weight(w, fmt):
    k, n = w.shape
    w = f64(np.asarray(w, np.float32).astype(ml_dtypes.bfloat16)).reshape(k // 32, 32, n)
    amax = np.abs(w).max(1)
    if fmt == "e4m3":
        byte = np.frexp(amax)[1] - 1 + 127 - 7
    else:
        mant, ex = np.frexp(amax / 6.0)
        byte = np.where(mant > 0.5, ex, ex - 1) + 127
    byte = np.clip(np.where(amax > 0, byte, 1), 1, 254)
    scaled = (w * np.exp2(127.0 - byte)[:, None, :]).reshape(k, n).astype(np.float32)
    by_word = np.ascontiguousarray(scaled.reshape(k // 512, 128, 4, n).transpose(0, 1, 3, 2))
    if fmt == "e4m3":
        words = by_word.astype(ml_dtypes.float8_e4m3fn).view(np.uint8)
    else:
        c = by_word.astype(ml_dtypes.float4_e2m1fn).view(np.uint8) & 0xF
        words = (c[..., 0::2] | (c[..., 1::2] << 4)).reshape(k // 512, 128, 2 * n)
    return np.ascontiguousarray(words), np.ascontiguousarray(byte.astype(np.uint8).reshape(k // 512, 16, n))


def unpack_weight(words, scales, fmt):
    g, _, n = scales.shape
    words = np.ascontiguousarray(words).reshape(g, 128, n, -1)
    if fmt == "e4m3":
        vals = words.view(ml_dtypes.float8_e4m3fn).astype(np.float64)
    else:
        nib = np.empty((g, 128, n, 4), np.uint8)
        nib[..., 0::2] = words & 0xF
        nib[..., 1::2] = words >> 4
        vals = E2M1[nib]
    vals = vals * np.repeat(np.exp2(scales.astype(np.float64) - 127.0), 8, axis=1)[..., None]
    return vals.transpose(0, 1, 3, 2).reshape(g * 512, n)


D, E, T, I, Q, G = 512, 512, 2048, 512, 128, 64


def setup_inputs():
    n = np.random.standard_normal
    idx = np.random.permutation(T)[:I]
    fd = mx_kscale(D)
    fe = mx_kscale(E)
    fi = mx_kscale(I)
    ti = np.ones(T)
    ti[idx] = fi
    keysp = pack_weight(n((D, T)) / fd[:, None], "e4m3")
    valsp = pack_weight(n((E, T)) / fe[:, None], "e4m3")
    return {
        "query": (n((D, Q)) * 0.6 / np.sqrt(D) * fd[:, None]).astype(np.float32),
        "keys_words": keysp[0],
        "keys_scales": keysp[1],
        "pen": (np.random.uniform(10.0, 40.0, (Q, 1))).astype(np.float32),
        "gout": (n((E, Q)) * 1 / np.sqrt(E) * fe[:, None]).astype(np.float32),
        "vals_words": valsp[0],
        "vals_scales": valsp[1],
        "fs": (np.random.uniform(128.0, 512.0, (1, I)) * fi).astype(np.float32),
        "keyrows": (n((D, T)) / ti).astype(np.float32),
        "res": (n((Q, D)) * 4.0).astype(np.float32),
        "offs": striped(idx),
    }


def reference(query, keys_words, keys_scales, pen, gout, vals_words, vals_scales, fs, keyrows, res, offs):
    idx = unstriped(offs)
    keysu = unpack_weight(keys_words, keys_scales, "e4m3")
    valsu = unpack_weight(vals_words, vals_scales, "e4m3")
    queryq = mxq(f64(query), 0, "e4m3")
    keysidxg = keysu[:, idx]
    a = queryq.T @ keysidxg
    p = np.exp(a - np.max(a, axis=1, keepdims=True))
    z = np.sum(p, axis=1, keepdims=True)
    goutq = mxq(f64(gout), 0, "e4m3")
    valsidxg = valsu[:, idx]
    c0 = goutq.T @ valsidxg
    s = p.reshape(Q, G, I // G).sum(axis=2) / z
    ds = f64(pen) * (-1.0) * s * 2.0
    e1 = ds / z
    r1 = np.repeat(e1, I // G, axis=1)
    dz = np.sum(ds * p.reshape(Q, G, I // G).sum(axis=2) / np.square(z) * (-1.0), axis=1, keepdims=True) - np.sum(p * c0, axis=1, keepdims=True) / np.square(z)
    dp = 1.0 / z * c0 + r1 + dz
    da = dp * p
    gs = da * f64(fs)
    gt1 = gs.T
    kt = f64(keyrows)[:, idx].T
    gt1q = mxq(gt1, 0, "e4m3")
    ktq = mxq(kt, 0, "e4m3")
    gq = gt1q.T @ ktq
    y = gq + f64(res)
    return y

@@ -1,0 +1,210 @@
+from contextlib import ExitStack
+
+import concourse.mybir as mybir
+from concourse.masks import make_identity
+
+F32 = mybir.dt.float32
+BF16 = mybir.dt.bfloat16
+I32 = mybir.dt.int32
+U32 = mybir.dt.uint32
+U16 = mybir.dt.uint16
+U8 = mybir.dt.uint8
+FP8X4 = mybir.dt.float8_e4m3fn_x4
+ALU = mybir.AluOpType
+ACT = mybir.ActivationFunctionType
+AXIS = mybir.AxisListType
+
+P = 128
+PACK = 4
+D = 512
+T = 2048
+SLOTS = 512
+Q = 128
+PAGE = 8
+PAGES = SLOTS // PAGE
+QUADS = 4
+FLOPS = 3 * 2 * Q * SLOTS * D
+
+
+def tile_attend_bcrowding_q_kernel(
+    tc, query, keys_words, keys_scales, pen, gout, vals_words, vals_scales, fs, keyrows, res, offs, out
+):
+    nc = tc.nc
+    with ExitStack() as ctx:
+        sb = ctx.enter_context(tc.tile_pool(name="sb", bufs=1))
+        ps = ctx.enter_context(tc.psum_pool(name="ps", bufs=1))
+
+        def sbuf(name, shape, dtype, after=None):
+            return sb.tile(shape, dtype, name=name, tag=after or name, align_bytes=64)
+
+        offsets = sbuf("offsets", [P, SLOTS // 16], U16)
+        key_bytes = sbuf("key_bytes", [P, T], U8)
+        val_bytes = sbuf("val_bytes", [P, T], U8)
+        identity = sbuf("identity", [P, P], F32)
+        nc.gpsimd.memset(key_bytes[:].bitcast(I32), 0)
+        nc.vector.memset(val_bytes[:].bitcast(I32), 0)
+        make_identity(nc, identity[:])
+
+        def load_bytes(queue, tile, scales):
+            for quad in range(QUADS):
+                queue.dma_start(
+                    tile[:].bitcast(I32)[32 * quad : 32 * quad + 4, :],
+                    scales[0].bitcast(I32)[4 * quad : 4 * quad + 4, :],
+                )
+
+        def load_words(name, words):
+            tile = sbuf(name, [P, T], U32)
+            nc.sync.dma_start(tile[:].bitcast(I32), words[0].rearrange("p n t -> p (n t)").bitcast(I32))
+            return tile
+
+        def load_columns(name, src):
+            tile = sbuf(name, [P, PACK, Q], F32)
+            nc.sync.dma_start(tile[:], src.rearrange("(p t) q -> p t q", t=PACK))
+            return tile
+
+        nc.sync.dma_start(offsets[:], offs)
+        key_pool = load_words("key_pool", keys_words)
+        load_bytes(nc.scalar, key_bytes, keys_scales)
+        query_raw = load_columns("query_raw", query)
+        val_pool = load_words("val_pool", vals_words)
+        load_bytes(nc.sync, val_bytes, vals_scales)
+        gout_raw = load_columns("gout_raw", gout)
+        fs_cols = sbuf("fs_cols", [P, PACK], F32)
+        nc.gpsimd.dma_start(fs_cols[:], fs.rearrange("o (p t) -> (o p) t", t=PACK))
+        pen_col = sbuf("pen_col", [P, 1], F32)
+        nc.gpsimd.dma_start(pen_col[:], pen)
+        row_pools = []
+        for j in range(D // P):
+            row_pool = sbuf("row_pool%d" % j, [P, T], F32)
+            nc.sync.dma_start(row_pool[:], keyrows[j * P : (j + 1) * P, :])
+            row_pools.append(row_pool)
+        res_sb = sbuf("res_sb", [P, D], F32)
+        nc.sync.dma_start(res_sb[:], res)
+
+        def quantise(name, woven, width, after=None):
+            codes = sbuf(name + "_codes", [P, width], U32, after)
+            scales = sbuf(name + "_scales", [P, width], U8)
+            nc.vector.quantize_mx(out=codes[:].bitcast(FP8X4), scales=scales[:], in_=woven[:])
+            return codes, scales
+
+        def quantise_columns(name, raw, after=None):
+            woven = sbuf(name + "_woven", [P, Q * PACK], BF16, after)
+            nc.scalar.activation(
+                woven[:].rearrange("p (q t) -> p q t", t=PACK), raw[:].rearrange("p t q -> p q t"), ACT.Copy
+            )
+            return quantise(name, woven, Q)
+
+        def gather(name, pool, dtype, after=None):
+            picked = sbuf(name, [P, SLOTS], dtype, after)
+            nc.vector.tensor_copy(picked[:], pool[:].indirect(offsets[:]))
+            return picked
+
+        def product(bank, lhs_codes, lhs_scales, rhs_codes, rhs_scales):
+            nc.tensor.matmul_mx(
+                out=bank,
+                lhsT=lhs_codes.bitcast(FP8X4),
+                lhsT_scale=lhs_scales,
+                rhs=rhs_codes.bitcast(FP8X4),
+                rhs_scale=rhs_scales,
+                start=True,
+                stop=True,
+            )
+
+        def turn(name, rows, woven):
+            turned = ps.tile([P, 2, P], F32, name=name + "_turned", tag="turned", bufs=3)
+            words = rows[:].bitcast(F32)
+            for half in range(2):
+                nc.tensor.transpose(turned[:, half, :], words[:, half : SLOTS // 2 : 2], identity[:])
+            nc.scalar.copy(
+                woven.bitcast(F32).rearrange("p (c h) -> p c h", h=2), turned[:].rearrange("p h c -> p c h")
+            )
+
+        key_scales = gather("key_scales", key_bytes, U8)
+        query_codes, query_scales = quantise_columns("query", query_raw)
+        key_codes = gather("key_codes", key_pool, U32, after="key_bytes")
+        scores = ps.tile([P, SLOTS], F32, name="scores")
+        product(scores[:], query_codes[:], query_scales[:], key_codes[:], key_scales[:])
+
+        neg_max = sbuf("neg_max", [P, 1], F32)
+        nc.vector.tensor_reduce(neg_max[:], scores[:], AXIS.X, ALU.max, negate=True)
+        weights = sbuf("weights", [P, SLOTS], F32)
+        total = sbuf("total", [P, 1], F32)
+        nc.scalar.activation(weights[:], scores[:], ACT.Exp, bias=neg_max[:], scale=1.0, accum_out=total[:])
+
+        val_codes = gather("val_codes", val_pool, U32, after="key_bytes")
+        val_scales = gather("val_scales", val_bytes, U8, after="key_scales")
+        gout_codes, gout_scales = quantise_columns("gout", gout_raw, after="neg_max")
+        reads = ps.tile([P, SLOTS], F32, name="reads")
+        product(reads[:], gout_codes[:], gout_scales[:], val_codes[:], val_scales[:])
+
+        fs_rows = ps.tile([P, PACK, P], F32, name="fs_rows")
+        for t in range(PACK):
+            nc.tensor.transpose(fs_rows[:, t, :], fs_cols[:, t : t + 1].to_broadcast([P, P]), identity[:])
+
+        rounded_pool = sbuf("rounded_pool", [P, T], BF16, after="gout_raw")
+        nc.scalar.activation(rounded_pool[:], row_pools[0][:], ACT.Copy)
+        first_rows = sbuf("first_rows", [P, SLOTS], BF16)
+        nc.scalar.activation(first_rows[:], rounded_pool[:].indirect(offsets[:]), ACT.Copy)
+
+        inv_total = sbuf("inv_total", [P, 1], F32)
+        nc.vector.reciprocal(inv_total[:], total[:])
+        page_sums = sbuf("page_sums", [P, PAGES], F32)
+        nc.vector.tensor_reduce(page_sums[:], weights[:].rearrange("p (g j) -> p g j", j=PAGE), AXIS.X, ALU.add)
+        page_factor = sbuf("page_factor", [P, 1], F32)
+        nc.vector.tensor_scalar(page_factor[:], inv_total[:], pen_col[:], -2.0, ALU.mult, ALU.mult)
+        scaled_shares = sbuf("scaled_shares", [P, SLOTS], F32)
+        nc.vector.scalar_tensor_tensor(
+            scaled_shares[:].rearrange("p (s t) -> p s t", t=PACK),
+            weights[:].rearrange("p (s t) -> p s t", t=PACK),
+            inv_total[:],
+            fs_rows[:].rearrange("p t s -> p s t"),
+            ALU.mult,
+            ALU.mult,
+        )
+        share_grad = sbuf("share_grad", [P, SLOTS], F32)
+        nc.vector.scalar_tensor_tensor(
+            share_grad[:].rearrange("p (g j) -> p g j", j=PAGE),
+            page_sums[:].unsqueeze(2).to_broadcast([P, PAGES, PAGE]),
+            page_factor[:],
+            reads[:].rearrange("p (g j) -> p g j", j=PAGE),
+            ALU.mult,
+            ALU.add,
+        )
+        rows1 = gather("rows1", row_pools[1], BF16, after="page_sums")
+        weighted = sbuf("weighted", [P, SLOTS], F32)
+        mean_grad = sbuf("mean_grad", [P, 1], F32)
+        nc.vector.scalar_tensor_tensor(
+            weighted[:], share_grad[:], inv_total[:], weights[:], ALU.mult, ALU.mult, accum_out=mean_grad[:]
+        )
+        rows2 = gather("rows2", row_pools[2], BF16, after="weights")
+        score_grad = sbuf("score_grad", [P, SLOTS], BF16)
+        nc.vector.scalar_tensor_tensor(
+            score_grad[:], share_grad[:], mean_grad[:], scaled_shares[:], ALU.subtract, ALU.mult
+        )
+
+        early_woven = sbuf("early_woven", [P, 4 * SLOTS], BF16)
+        last_woven = sbuf("last_woven", [P, SLOTS], BF16)
+        turn("rows0", first_rows, early_woven[:, SLOTS : 2 * SLOTS])
+        turn("rows1", rows1, early_woven[:, 2 * SLOTS : 3 * SLOTS])
+        turn("rows2", rows2, early_woven[:, 3 * SLOTS : 4 * SLOTS])
+        turn("grad", score_grad, early_woven[:, 0:SLOTS])
+        rows3 = gather("rows3", row_pools[3], BF16, after="mean_grad")
+        turn("rows3", rows3, last_woven[:])
+        early_codes, early_scales = quantise("early", early_woven, 4 * P, after="row_pool3")
+        last_codes, last_scales = quantise("last", last_woven, P)
+
+        early_sums = ps.tile([P, 3 * P], F32, name="early_sums")
+        for lo, hi in ((0, 2 * P), (2 * P, 3 * P)):
+            product(
+                early_sums[:, lo:hi],
+                early_codes[:, 0:P],
+                early_scales[:, 0:P],
+                early_codes[:, P + lo : P + hi],
+                early_scales[:, P + lo : P + hi],
+            )
+        last_sums = ps.tile([P, P], F32, name="last_sums")
+        product(last_sums[:], early_codes[:, 0:P], early_scales[:, 0:P], last_codes[:], last_scales[:])
+        for name, sums, cols in (("early", early_sums, slice(0, 3 * P)), ("last", last_sums, slice(3 * P, D))):
+            result = sbuf(name + "_result", [P, cols.stop - cols.start], F32)
+            nc.vector.tensor_tensor(result[:], sums[:], res_sb[:, cols], ALU.add)
+            nc.sync.dma_start(out[:, cols], result[:])

@@ -45,9 +45,9 @@ def tile_attend_bcrowding_q_kernel(
         nc.vector.memset(val_bytes[:].bitcast(I32), 0)
         make_identity(nc, identity[:])
 
-        def load_bytes(queue, tile, scales):
+        def load_bytes(tile, scales):
             for quad in range(QUADS):
-                queue.dma_start(
+                nc.sync.dma_start(
                     tile[:].bitcast(I32)[32 * quad : 32 * quad + 4, :],
                     scales[0].bitcast(I32)[4 * quad : 4 * quad + 4, :],
                 )
@@ -63,21 +63,23 @@ def tile_attend_bcrowding_q_kernel(
             return tile
 
         nc.sync.dma_start(offsets[:], offs)
-        key_pool = load_words("key_pool", keys_words)
-        load_bytes(nc.scalar, key_bytes, keys_scales)
-        query_raw = load_columns("query_raw", query)
-        val_pool = load_words("val_pool", vals_words)
-        load_bytes(nc.sync, val_bytes, vals_scales)
-        gout_raw = load_columns("gout_raw", gout)
         fs_cols = sbuf("fs_cols", [P, PACK], F32)
-        nc.gpsimd.dma_start(fs_cols[:], fs.rearrange("o (p t) -> (o p) t", t=PACK))
+        nc.sync.dma_start(fs_cols[:], fs.rearrange("o (p t) -> (o p) t", t=PACK))
+        key_pool = load_words("key_pool", keys_words)
+        load_bytes(key_bytes, keys_scales)
+        query_raw = load_columns("query_raw", query)
+        gout_raw = load_columns("gout_raw", gout)
+        val_pool = load_words("val_pool", vals_words)
+        load_bytes(val_bytes, vals_scales)
+
+        def load_rows(j):
+            tile = sbuf("row_pool%d" % j, [P, T], F32)
+            nc.sync.dma_start(tile[:], keyrows[j * P : (j + 1) * P, :])
+            return tile
+
         pen_col = sbuf("pen_col", [P, 1], F32)
         nc.gpsimd.dma_start(pen_col[:], pen)
-        row_pools = []
-        for j in range(D // P):
-            row_pool = sbuf("row_pool%d" % j, [P, T], F32)
-            nc.sync.dma_start(row_pool[:], keyrows[j * P : (j + 1) * P, :])
-            row_pools.append(row_pool)
+        row_pools = [load_rows(j) for j in range(D // P)]
         res_sb = sbuf("res_sb", [P, D], F32)
         nc.sync.dma_start(res_sb[:], res)
 
@@ -119,9 +121,14 @@ def tile_attend_bcrowding_q_kernel(
                 woven.bitcast(F32).rearrange("p (c h) -> p c h", h=2), turned[:].rearrange("p h c -> p c h")
             )
 
+        fs_rows = ps.tile([P, PACK, P], F32, name="fs_rows")
+        for t in range(PACK):
+            nc.tensor.transpose(fs_rows[:, t, :], fs_cols[:, t : t + 1].to_broadcast([P, P]), identity[:])
+
+        key_codes = gather("key_codes", key_pool, U32)
         key_scales = gather("key_scales", key_bytes, U8)
         query_codes, query_scales = quantise_columns("query", query_raw)
-        key_codes = gather("key_codes", key_pool, U32, after="key_bytes")
+        gout_codes, gout_scales = quantise_columns("gout", gout_raw)
         scores = ps.tile([P, SLOTS], F32, name="scores")
         product(scores[:], query_codes[:], query_scales[:], key_codes[:], key_scales[:])
 
@@ -131,32 +138,27 @@ def tile_attend_bcrowding_q_kernel(
         total = sbuf("total", [P, 1], F32)
         nc.scalar.activation(weights[:], scores[:], ACT.Exp, bias=neg_max[:], scale=1.0, accum_out=total[:])
 
-        val_codes = gather("val_codes", val_pool, U32, after="key_bytes")
+        val_codes = gather("val_codes", val_pool, U32, after="key_codes")
         val_scales = gather("val_scales", val_bytes, U8, after="key_scales")
-        gout_codes, gout_scales = quantise_columns("gout", gout_raw, after="neg_max")
         reads = ps.tile([P, SLOTS], F32, name="reads")
         product(reads[:], gout_codes[:], gout_scales[:], val_codes[:], val_scales[:])
 
-        fs_rows = ps.tile([P, PACK, P], F32, name="fs_rows")
-        for t in range(PACK):
-            nc.tensor.transpose(fs_rows[:, t, :], fs_cols[:, t : t + 1].to_broadcast([P, P]), identity[:])
-
-        rounded_pool = sbuf("rounded_pool", [P, T], BF16, after="gout_raw")
+        rounded_pool = sbuf("rounded_pool", [P, T], BF16, after="neg_max")
         nc.scalar.activation(rounded_pool[:], row_pools[0][:], ACT.Copy)
         first_rows = sbuf("first_rows", [P, SLOTS], BF16)
         nc.scalar.activation(first_rows[:], rounded_pool[:].indirect(offsets[:]), ACT.Copy)
 
-        inv_total = sbuf("inv_total", [P, 1], F32)
-        nc.vector.reciprocal(inv_total[:], total[:])
-        page_sums = sbuf("page_sums", [P, PAGES], F32)
-        nc.vector.tensor_reduce(page_sums[:], weights[:].rearrange("p (g j) -> p g j", j=PAGE), AXIS.X, ALU.add)
+        stats = sbuf("stats", [P, PAGES + 1], F32, after="val_bytes")
+        page_sums, inv_total = stats[:, 0:PAGES], stats[:, PAGES : PAGES + 1]
+        nc.vector.reciprocal(inv_total, total[:])
+        nc.vector.tensor_reduce(page_sums, weights[:].rearrange("p (g j) -> p g j", j=PAGE), AXIS.X, ALU.add)
         page_factor = sbuf("page_factor", [P, 1], F32)
-        nc.vector.tensor_scalar(page_factor[:], inv_total[:], pen_col[:], -2.0, ALU.mult, ALU.mult)
+        nc.vector.tensor_scalar(page_factor[:], inv_total, pen_col[:], -2.0, ALU.mult, ALU.mult)
         scaled_shares = sbuf("scaled_shares", [P, SLOTS], F32)
         nc.vector.scalar_tensor_tensor(
             scaled_shares[:].rearrange("p (s t) -> p s t", t=PACK),
             weights[:].rearrange("p (s t) -> p s t", t=PACK),
-            inv_total[:],
+            inv_total,
             fs_rows[:].rearrange("p t s -> p s t"),
             ALU.mult,
             ALU.mult,
@@ -164,19 +166,17 @@ def tile_attend_bcrowding_q_kernel(
         share_grad = sbuf("share_grad", [P, SLOTS], F32)
         nc.vector.scalar_tensor_tensor(
             share_grad[:].rearrange("p (g j) -> p g j", j=PAGE),
-            page_sums[:].unsqueeze(2).to_broadcast([P, PAGES, PAGE]),
+            page_sums.unsqueeze(2).to_broadcast([P, PAGES, PAGE]),
             page_factor[:],
             reads[:].rearrange("p (g j) -> p g j", j=PAGE),
             ALU.mult,
             ALU.add,
         )
-        rows1 = gather("rows1", row_pools[1], BF16, after="page_sums")
         weighted = sbuf("weighted", [P, SLOTS], F32)
         mean_grad = sbuf("mean_grad", [P, 1], F32)
         nc.vector.scalar_tensor_tensor(
-            weighted[:], share_grad[:], inv_total[:], weights[:], ALU.mult, ALU.mult, accum_out=mean_grad[:]
+            weighted[:], share_grad[:], inv_total, weights[:], ALU.mult, ALU.mult, accum_out=mean_grad[:]
         )
-        rows2 = gather("rows2", row_pools[2], BF16, after="weights")
         score_grad = sbuf("score_grad", [P, SLOTS], BF16)
         nc.vector.scalar_tensor_tensor(
             score_grad[:], share_grad[:], mean_grad[:], scaled_shares[:], ALU.subtract, ALU.mult
@@ -184,11 +184,13 @@ def tile_attend_bcrowding_q_kernel(
 
         early_woven = sbuf("early_woven", [P, 4 * SLOTS], BF16)
         last_woven = sbuf("last_woven", [P, SLOTS], BF16)
-        turn("rows0", first_rows, early_woven[:, SLOTS : 2 * SLOTS])
-        turn("rows1", rows1, early_woven[:, 2 * SLOTS : 3 * SLOTS])
-        turn("rows2", rows2, early_woven[:, 3 * SLOTS : 4 * SLOTS])
         turn("grad", score_grad, early_woven[:, 0:SLOTS])
-        rows3 = gather("rows3", row_pools[3], BF16, after="mean_grad")
+        turn("rows0", first_rows, early_woven[:, SLOTS : 2 * SLOTS])
+        rows1 = gather("rows1", row_pools[1], BF16, after="weights")
+        turn("rows1", rows1, early_woven[:, 2 * SLOTS : 3 * SLOTS])
+        rows2 = gather("rows2", row_pools[2], BF16, after="scaled_shares")
+        turn("rows2", rows2, early_woven[:, 3 * SLOTS : 4 * SLOTS])
+        rows3 = gather("rows3", row_pools[3], BF16, after="share_grad")
         turn("rows3", rows3, last_woven[:])
         early_codes, early_scales = quantise("early", early_woven, 4 * P, after="row_pool3")
         last_codes, last_scales = quantise("last", last_woven, P)
@@ -204,7 +206,10 @@ def tile_attend_bcrowding_q_kernel(
             )
         last_sums = ps.tile([P, P], F32, name="last_sums")
         product(last_sums[:], early_codes[:, 0:P], early_scales[:, 0:P], last_codes[:], last_scales[:])
-        for name, sums, cols in (("early", early_sums, slice(0, 3 * P)), ("last", last_sums, slice(3 * P, D))):
-            result = sbuf(name + "_result", [P, cols.stop - cols.start], F32)
+        for name, sums, cols, after in (
+            ("early", early_sums, slice(0, 3 * P), "last_woven"),
+            ("last", last_sums, slice(3 * P, D), None),
+        ):
+            result = sbuf(name + "_result", [P, cols.stop - cols.start], F32, after)
             nc.vector.tensor_tensor(result[:], sums[:], res_sb[:, cols], ALU.add)
             nc.sync.dma_start(out[:, cols], result[:])

@@ -134,11 +134,11 @@ def tile_attend_bcrowding_q_kernel(
 
         neg_max = sbuf("neg_max", [P, 1], F32)
         nc.vector.tensor_reduce(neg_max[:], scores[:], AXIS.X, ALU.max, negate=True)
-        weights = sbuf("weights", [P, SLOTS], F32)
+        val_codes = gather("val_codes", val_pool, U32, after="key_codes")
+        weights = sbuf("weights", [P, SLOTS], F32, after="val_pool")
         total = sbuf("total", [P, 1], F32)
         nc.scalar.activation(weights[:], scores[:], ACT.Exp, bias=neg_max[:], scale=1.0, accum_out=total[:])
 
-        val_codes = gather("val_codes", val_pool, U32, after="key_codes")
         val_scales = gather("val_scales", val_bytes, U8, after="key_scales")
         reads = ps.tile([P, SLOTS], F32, name="reads")
         product(reads[:], gout_codes[:], gout_scales[:], val_codes[:], val_scales[:])
@@ -148,8 +148,8 @@ def tile_attend_bcrowding_q_kernel(
         first_rows = sbuf("first_rows", [P, SLOTS], BF16)
         nc.scalar.activation(first_rows[:], rounded_pool[:].indirect(offsets[:]), ACT.Copy)
 
-        stats = sbuf("stats", [P, PAGES + 1], F32, after="val_bytes")
-        page_sums, inv_total = stats[:, 0:PAGES], stats[:, PAGES : PAGES + 1]
+        inv_total = sbuf("inv_total", [P, 1], F32)[:]
+        page_sums = sbuf("page_sums", [P, PAGES], F32)[:]
         nc.vector.reciprocal(inv_total, total[:])
         nc.vector.tensor_reduce(page_sums, weights[:].rearrange("p (g j) -> p g j", j=PAGE), AXIS.X, ALU.add)
         page_factor = sbuf("page_factor", [P, 1], F32)
@@ -172,7 +172,8 @@ def tile_attend_bcrowding_q_kernel(
             ALU.mult,
             ALU.add,
         )
-        weighted = sbuf("weighted", [P, SLOTS], F32)
+        rows1 = gather("rows1", row_pools[1], BF16)
+        weighted = sbuf("weighted", [P, SLOTS], F32, after="row_pool0")
         mean_grad = sbuf("mean_grad", [P, 1], F32)
         nc.vector.scalar_tensor_tensor(
             weighted[:], share_grad[:], inv_total, weights[:], ALU.mult, ALU.mult, accum_out=mean_grad[:]
@@ -186,7 +187,6 @@ def tile_attend_bcrowding_q_kernel(
         last_woven = sbuf("last_woven", [P, SLOTS], BF16)
         turn("grad", score_grad, early_woven[:, 0:SLOTS])
         turn("rows0", first_rows, early_woven[:, SLOTS : 2 * SLOTS])
-        rows1 = gather("rows1", row_pools[1], BF16, after="weights")
         turn("rows1", rows1, early_woven[:, 2 * SLOTS : 3 * SLOTS])
         rows2 = gather("rows2", row_pools[2], BF16, after="scaled_shares")
         turn("rows2", rows2, early_woven[:, 3 * SLOTS : 4 * SLOTS])

@@ -63,23 +63,21 @@ def tile_attend_bcrowding_q_kernel(
             return tile
 
         nc.sync.dma_start(offsets[:], offs)
-        fs_cols = sbuf("fs_cols", [P, PACK], F32)
-        nc.sync.dma_start(fs_cols[:], fs.rearrange("o (p t) -> (o p) t", t=PACK))
         key_pool = load_words("key_pool", keys_words)
         load_bytes(key_bytes, keys_scales)
         query_raw = load_columns("query_raw", query)
-        gout_raw = load_columns("gout_raw", gout)
         val_pool = load_words("val_pool", vals_words)
         load_bytes(val_bytes, vals_scales)
-
-        def load_rows(j):
-            tile = sbuf("row_pool%d" % j, [P, T], F32)
-            nc.sync.dma_start(tile[:], keyrows[j * P : (j + 1) * P, :])
-            return tile
-
+        gout_raw = load_columns("gout_raw", gout)
+        fs_cols = sbuf("fs_cols", [P, PACK], F32)
+        nc.sync.dma_start(fs_cols[:], fs.rearrange("o (p t) -> (o p) t", t=PACK))
         pen_col = sbuf("pen_col", [P, 1], F32)
         nc.gpsimd.dma_start(pen_col[:], pen)
-        row_pools = [load_rows(j) for j in range(D // P)]
+        row_pools = []
+        for j in range(D // P):
+            row_pool = sbuf("row_pool%d" % j, [P, T], F32)
+            nc.sync.dma_start(row_pool[:], keyrows[j * P : (j + 1) * P, :])
+            row_pools.append(row_pool)
         res_sb = sbuf("res_sb", [P, D], F32)
         nc.sync.dma_start(res_sb[:], res)
 
@@ -121,44 +119,44 @@ def tile_attend_bcrowding_q_kernel(
                 woven.bitcast(F32).rearrange("p (c h) -> p c h", h=2), turned[:].rearrange("p h c -> p c h")
             )
 
-        fs_rows = ps.tile([P, PACK, P], F32, name="fs_rows")
-        for t in range(PACK):
-            nc.tensor.transpose(fs_rows[:, t, :], fs_cols[:, t : t + 1].to_broadcast([P, P]), identity[:])
-
         key_codes = gather("key_codes", key_pool, U32)
         key_scales = gather("key_scales", key_bytes, U8)
         query_codes, query_scales = quantise_columns("query", query_raw)
-        gout_codes, gout_scales = quantise_columns("gout", gout_raw)
         scores = ps.tile([P, SLOTS], F32, name="scores")
         product(scores[:], query_codes[:], query_scales[:], key_codes[:], key_scales[:])
 
         neg_max = sbuf("neg_max", [P, 1], F32)
         nc.vector.tensor_reduce(neg_max[:], scores[:], AXIS.X, ALU.max, negate=True)
-        val_codes = gather("val_codes", val_pool, U32, after="key_codes")
-        weights = sbuf("weights", [P, SLOTS], F32, after="val_pool")
+        weights = sbuf("weights", [P, SLOTS], F32)
         total = sbuf("total", [P, 1], F32)
         nc.scalar.activation(weights[:], scores[:], ACT.Exp, bias=neg_max[:], scale=1.0, accum_out=total[:])
 
+        val_codes = gather("val_codes", val_pool, U32, after="key_codes")
         val_scales = gather("val_scales", val_bytes, U8, after="key_scales")
+        gout_codes, gout_scales = quantise_columns("gout", gout_raw, after="neg_max")
         reads = ps.tile([P, SLOTS], F32, name="reads")
         product(reads[:], gout_codes[:], gout_scales[:], val_codes[:], val_scales[:])
 
-        rounded_pool = sbuf("rounded_pool", [P, T], BF16, after="neg_max")
+        fs_rows = ps.tile([P, PACK, P], F32, name="fs_rows")
+        for t in range(PACK):
+            nc.tensor.transpose(fs_rows[:, t, :], fs_cols[:, t : t + 1].to_broadcast([P, P]), identity[:])
+
+        rounded_pool = sbuf("rounded_pool", [P, T], BF16, after="gout_raw")
         nc.scalar.activation(rounded_pool[:], row_pools[0][:], ACT.Copy)
         first_rows = sbuf("first_rows", [P, SLOTS], BF16)
         nc.scalar.activation(first_rows[:], rounded_pool[:].indirect(offsets[:]), ACT.Copy)
 
-        inv_total = sbuf("inv_total", [P, 1], F32)[:]
-        page_sums = sbuf("page_sums", [P, PAGES], F32)[:]
-        nc.vector.reciprocal(inv_total, total[:])
-        nc.vector.tensor_reduce(page_sums, weights[:].rearrange("p (g j) -> p g j", j=PAGE), AXIS.X, ALU.add)
+        inv_total = sbuf("inv_total", [P, 1], F32)
+        nc.vector.reciprocal(inv_total[:], total[:])
+        page_sums = sbuf("page_sums", [P, PAGES], F32)
+        nc.vector.tensor_reduce(page_sums[:], weights[:].rearrange("p (g j) -> p g j", j=PAGE), AXIS.X, ALU.add)
         page_factor = sbuf("page_factor", [P, 1], F32)
-        nc.vector.tensor_scalar(page_factor[:], inv_total, pen_col[:], -2.0, ALU.mult, ALU.mult)
+        nc.vector.tensor_scalar(page_factor[:], inv_total[:], pen_col[:], -2.0, ALU.mult, ALU.mult)
         scaled_shares = sbuf("scaled_shares", [P, SLOTS], F32)
         nc.vector.scalar_tensor_tensor(
             scaled_shares[:].rearrange("p (s t) -> p s t", t=PACK),
             weights[:].rearrange("p (s t) -> p s t", t=PACK),
-            inv_total,
+            inv_total[:],
             fs_rows[:].rearrange("p t s -> p s t"),
             ALU.mult,
             ALU.mult,
@@ -166,18 +164,19 @@ def tile_attend_bcrowding_q_kernel(
         share_grad = sbuf("share_grad", [P, SLOTS], F32)
         nc.vector.scalar_tensor_tensor(
             share_grad[:].rearrange("p (g j) -> p g j", j=PAGE),
-            page_sums.unsqueeze(2).to_broadcast([P, PAGES, PAGE]),
+            page_sums[:].unsqueeze(2).to_broadcast([P, PAGES, PAGE]),
             page_factor[:],
             reads[:].rearrange("p (g j) -> p g j", j=PAGE),
             ALU.mult,
             ALU.add,
         )
-        rows1 = gather("rows1", row_pools[1], BF16)
-        weighted = sbuf("weighted", [P, SLOTS], F32, after="row_pool0")
+        rows1 = gather("rows1", row_pools[1], BF16, after="page_sums")
+        weighted = sbuf("weighted", [P, SLOTS], F32)
         mean_grad = sbuf("mean_grad", [P, 1], F32)
         nc.vector.scalar_tensor_tensor(
-            weighted[:], share_grad[:], inv_total, weights[:], ALU.mult, ALU.mult, accum_out=mean_grad[:]
+            weighted[:], share_grad[:], inv_total[:], weights[:], ALU.mult, ALU.mult, accum_out=mean_grad[:]
         )
+        rows2 = gather("rows2", row_pools[2], BF16, after="weights")
         score_grad = sbuf("score_grad", [P, SLOTS], BF16)
         nc.vector.scalar_tensor_tensor(
             score_grad[:], share_grad[:], mean_grad[:], scaled_shares[:], ALU.subtract, ALU.mult
@@ -185,12 +184,11 @@ def tile_attend_bcrowding_q_kernel(
 
         early_woven = sbuf("early_woven", [P, 4 * SLOTS], BF16)
         last_woven = sbuf("last_woven", [P, SLOTS], BF16)
-        turn("grad", score_grad, early_woven[:, 0:SLOTS])
         turn("rows0", first_rows, early_woven[:, SLOTS : 2 * SLOTS])
         turn("rows1", rows1, early_woven[:, 2 * SLOTS : 3 * SLOTS])
-        rows2 = gather("rows2", row_pools[2], BF16, after="scaled_shares")
         turn("rows2", rows2, early_woven[:, 3 * SLOTS : 4 * SLOTS])
-        rows3 = gather("rows3", row_pools[3], BF16, after="share_grad")
+        turn("grad", score_grad, early_woven[:, 0:SLOTS])
+        rows3 = gather("rows3", row_pools[3], BF16, after="mean_grad")
         turn("rows3", rows3, last_woven[:])
         early_codes, early_scales = quantise("early", early_woven, 4 * P, after="row_pool3")
         last_codes, last_scales = quantise("last", last_woven, P)
@@ -206,10 +204,7 @@ def tile_attend_bcrowding_q_kernel(
             )
         last_sums = ps.tile([P, P], F32, name="last_sums")
         product(last_sums[:], early_codes[:, 0:P], early_scales[:, 0:P], last_codes[:], last_scales[:])
-        for name, sums, cols, after in (
-            ("early", early_sums, slice(0, 3 * P), "last_woven"),
-            ("last", last_sums, slice(3 * P, D), None),
-        ):
-            result = sbuf(name + "_result", [P, cols.stop - cols.start], F32, after)
+        for name, sums, cols in (("early", early_sums, slice(0, 3 * P)), ("last", last_sums, slice(3 * P, D))):
+            result = sbuf(name + "_result", [P, cols.stop - cols.start], F32)
             nc.vector.tensor_tensor(result[:], sums[:], res_sb[:, cols], ALU.add)
             nc.sync.dma_start(out[:, cols], result[:])

from contextlib import ExitStack

import concourse.mybir as mybir
from concourse.masks import make_identity

F32 = mybir.dt.float32
BF16 = mybir.dt.bfloat16
I32 = mybir.dt.int32
U32 = mybir.dt.uint32
U16 = mybir.dt.uint16
U8 = mybir.dt.uint8
FP8X4 = mybir.dt.float8_e4m3fn_x4
ALU = mybir.AluOpType
ACT = mybir.ActivationFunctionType
AXIS = mybir.AxisListType

P = 128
PACK = 4
D = 512
T = 2048
SLOTS = 512
Q = 128
PAGE = 8
PAGES = SLOTS // PAGE
QUADS = 4
FLOPS = 3 * 2 * Q * SLOTS * D


def tile_attend_bcrowding_q_kernel(
    tc, query, keys_words, keys_scales, pen, gout, vals_words, vals_scales, fs, keyrows, res, offs, out
):
    nc = tc.nc
    with ExitStack() as ctx:
        sb = ctx.enter_context(tc.tile_pool(name="sb", bufs=1))
        ps = ctx.enter_context(tc.psum_pool(name="ps", bufs=1))

        def sbuf(name, shape, dtype, after=None):
            return sb.tile(shape, dtype, name=name, tag=after or name, align_bytes=64)

        offsets = sbuf("offsets", [P, SLOTS // 16], U16)
        key_bytes = sbuf("key_bytes", [P, T], U8)
        val_bytes = sbuf("val_bytes", [P, T], U8)
        identity = sbuf("identity", [P, P], F32)
        nc.gpsimd.memset(key_bytes[:].bitcast(I32), 0)
        nc.vector.memset(val_bytes[:].bitcast(I32), 0)
        make_identity(nc, identity[:])

        def load_bytes(tile, scales):
            for quad in range(QUADS):
                nc.sync.dma_start(
                    tile[:].bitcast(I32)[32 * quad : 32 * quad + 4, :],
                    scales[0].bitcast(I32)[4 * quad : 4 * quad + 4, :],
                )

        def load_words(name, words):
            tile = sbuf(name, [P, T], U32)
            nc.sync.dma_start(tile[:].bitcast(I32), words[0].rearrange("p n t -> p (n t)").bitcast(I32))
            return tile

        def load_columns(name, src):
            tile = sbuf(name, [P, PACK, Q], F32)
            nc.sync.dma_start(tile[:], src.rearrange("(p t) q -> p t q", t=PACK))
            return tile

        nc.sync.dma_start(offsets[:], offs)
        key_pool = load_words("key_pool", keys_words)
        load_bytes(key_bytes, keys_scales)
        query_raw = load_columns("query_raw", query)
        val_pool = load_words("val_pool", vals_words)
        load_bytes(val_bytes, vals_scales)
        gout_raw = load_columns("gout_raw", gout)
        fs_cols = sbuf("fs_cols", [P, PACK], F32)
        nc.sync.dma_start(fs_cols[:], fs.rearrange("o (p t) -> (o p) t", t=PACK))
        pen_col = sbuf("pen_col", [P, 1], F32)
        nc.gpsimd.dma_start(pen_col[:], pen)
        row_pools = []
        for j in range(D // P):
            row_pool = sbuf("row_pool%d" % j, [P, T], F32)
            nc.sync.dma_start(row_pool[:], keyrows[j * P : (j + 1) * P, :])
            row_pools.append(row_pool)
        res_sb = sbuf("res_sb", [P, D], F32)
        nc.sync.dma_start(res_sb[:], res)

        def quantise(name, woven, width, after=None):
            codes = sbuf(name + "_codes", [P, width], U32, after)
            scales = sbuf(name + "_scales", [P, width], U8)
            nc.vector.quantize_mx(out=codes[:].bitcast(FP8X4), scales=scales[:], in_=woven[:])
            return codes, scales

        def quantise_columns(name, raw, after=None):
            woven = sbuf(name + "_woven", [P, Q * PACK], BF16, after)
            nc.scalar.activation(
                woven[:].rearrange("p (q t) -> p q t", t=PACK), raw[:].rearrange("p t q -> p q t"), ACT.Copy
            )
            return quantise(name, woven, Q)

        def gather(name, pool, dtype, after=None):
            picked = sbuf(name, [P, SLOTS], dtype, after)
            nc.vector.tensor_copy(picked[:], pool[:].indirect(offsets[:]))
            return picked

        def product(bank, lhs_codes, lhs_scales, rhs_codes, rhs_scales):
            nc.tensor.matmul_mx(
                out=bank,
                lhsT=lhs_codes.bitcast(FP8X4),
                lhsT_scale=lhs_scales,
                rhs=rhs_codes.bitcast(FP8X4),
                rhs_scale=rhs_scales,
                start=True,
                stop=True,
            )

        def turn(name, rows, woven):
            turned = ps.tile([P, 2, P], F32, name=name + "_turned", tag="turned", bufs=3)
            words = rows[:].bitcast(F32)
            for half in range(2):
                nc.tensor.transpose(turned[:, half, :], words[:, half : SLOTS // 2 : 2], identity[:])
            nc.scalar.copy(
                woven.bitcast(F32).rearrange("p (c h) -> p c h", h=2), turned[:].rearrange("p h c -> p c h")
            )

        key_codes = gather("key_codes", key_pool, U32)
        key_scales = gather("key_scales", key_bytes, U8)
        query_codes, query_scales = quantise_columns("query", query_raw)
        scores = ps.tile([P, SLOTS], F32, name="scores")
        product(scores[:], query_codes[:], query_scales[:], key_codes[:], key_scales[:])

        neg_max = sbuf("neg_max", [P, 1], F32)
        nc.vector.tensor_reduce(neg_max[:], scores[:], AXIS.X, ALU.max, negate=True)
        weights = sbuf("weights", [P, SLOTS], F32)
        total = sbuf("total", [P, 1], F32)
        nc.scalar.activation(weights[:], scores[:], ACT.Exp, bias=neg_max[:], scale=1.0, accum_out=total[:])

        val_codes = gather("val_codes", val_pool, U32, after="key_codes")
        val_scales = gather("val_scales", val_bytes, U8, after="key_scales")
        gout_codes, gout_scales = quantise_columns("gout", gout_raw, after="neg_max")
        reads = ps.tile([P, SLOTS], F32, name="reads")
        product(reads[:], gout_codes[:], gout_scales[:], val_codes[:], val_scales[:])

        fs_rows = ps.tile([P, PACK, P], F32, name="fs_rows")
        for t in range(PACK):
            nc.tensor.transpose(fs_rows[:, t, :], fs_cols[:, t : t + 1].to_broadcast([P, P]), identity[:])

        rounded_pool = sbuf("rounded_pool", [P, T], BF16, after="gout_raw")
        nc.scalar.activation(rounded_pool[:], row_pools[0][:], ACT.Copy)
        first_rows = sbuf("first_rows", [P, SLOTS], BF16)
        nc.scalar.activation(first_rows[:], rounded_pool[:].indirect(offsets[:]), ACT.Copy)

        inv_total = sbuf("inv_total", [P, 1], F32)
        nc.vector.reciprocal(inv_total[:], total[:])
        page_sums = sbuf("page_sums", [P, PAGES], F32)
        nc.vector.tensor_reduce(page_sums[:], weights[:].rearrange("p (g j) -> p g j", j=PAGE), AXIS.X, ALU.add)
        page_factor = sbuf("page_factor", [P, 1], F32)
        nc.vector.tensor_scalar(page_factor[:], inv_total[:], pen_col[:], -2.0, ALU.mult, ALU.mult)
        scaled_shares = sbuf("scaled_shares", [P, SLOTS], F32)
        nc.vector.scalar_tensor_tensor(
            scaled_shares[:].rearrange("p (s t) -> p s t", t=PACK),
            weights[:].rearrange("p (s t) -> p s t", t=PACK),
            inv_total[:],
            fs_rows[:].rearrange("p t s -> p s t"),
            ALU.mult,
            ALU.mult,
        )
        share_grad = sbuf("share_grad", [P, SLOTS], F32)
        nc.vector.scalar_tensor_tensor(
            share_grad[:].rearrange("p (g j) -> p g j", j=PAGE),
            page_sums[:].unsqueeze(2).to_broadcast([P, PAGES, PAGE]),
            page_factor[:],
            reads[:].rearrange("p (g j) -> p g j", j=PAGE),
            ALU.mult,
            ALU.add,
        )
        rows1 = gather("rows1", row_pools[1], BF16, after="page_sums")
        weighted = sbuf("weighted", [P, SLOTS], F32)
        mean_grad = sbuf("mean_grad", [P, 1], F32)
        nc.vector.scalar_tensor_tensor(
            weighted[:], share_grad[:], inv_total[:], weights[:], ALU.mult, ALU.mult, accum_out=mean_grad[:]
        )
        rows2 = gather("rows2", row_pools[2], BF16, after="weights")
        score_grad = sbuf("score_grad", [P, SLOTS], BF16)
        nc.vector.scalar_tensor_tensor(
            score_grad[:], share_grad[:], mean_grad[:], scaled_shares[:], ALU.subtract, ALU.mult
        )

        early_woven = sbuf("early_woven", [P, 4 * SLOTS], BF16)
        last_woven = sbuf("last_woven", [P, SLOTS], BF16)
        turn("rows0", first_rows, early_woven[:, SLOTS : 2 * SLOTS])
        turn("rows1", rows1, early_woven[:, 2 * SLOTS : 3 * SLOTS])
        turn("rows2", rows2, early_woven[:, 3 * SLOTS : 4 * SLOTS])
        turn("grad", score_grad, early_woven[:, 0:SLOTS])
        rows3 = gather("rows3", row_pools[3], BF16, after="mean_grad")
        turn("rows3", rows3, last_woven[:])
        early_codes, early_scales = quantise("early", early_woven, 4 * P, after="row_pool3")
        last_codes, last_scales = quantise("last", last_woven, P)

        early_sums = ps.tile([P, 3 * P], F32, name="early_sums")
        for lo, hi in ((0, 2 * P), (2 * P, 3 * P)):
            product(
                early_sums[:, lo:hi],
                early_codes[:, 0:P],
                early_scales[:, 0:P],
                early_codes[:, P + lo : P + hi],
                early_scales[:, P + lo : P + hi],
            )
        last_sums = ps.tile([P, P], F32, name="last_sums")
        product(last_sums[:], early_codes[:, 0:P], early_scales[:, 0:P], last_codes[:], last_scales[:])
        for name, sums, cols in (("early", early_sums, slice(0, 3 * P)), ("last", last_sums, slice(3 * P, D))):
            result = sbuf(name + "_result", [P, cols.stop - cols.start], F32)
            nc.vector.tensor_tensor(result[:], sums[:], res_sb[:, cols], ALU.add)
            nc.sync.dma_start(out[:, cols], result[:])
